import numpy as np, ml_dtypes
CORES = [2,3,42,43,82,83,122,123]
N = 8
import mx_ref
BF = ml_dtypes.bfloat16
def entries(a):
    return np.ascontiguousarray(a.T).reshape(-1)
def table(e):
    return np.ascontiguousarray(np.reshape(e, (-1, 16)).T).astype(np.int32)
def cols(t, e):
    v = np.concatenate([t.reshape(128, -1, 4), np.zeros((128, 1, 4), BF)], axis=1)
    return np.ascontiguousarray(v[:, e]).reshape(128, -1)
def f(rng, *shape):
    return mx_ref.flush((rng.standard_normal(shape, dtype=np.float32) * np.exp2(rng.integers(-2, 3, shape[:-1] + (1,)))).astype(BF))
def wide(rng, *shape, cols=0):
    v = rng.standard_normal(shape, dtype=np.float32) * np.exp2(rng.integers(-12, 13, shape)).astype(np.float32)
    if cols: v *= np.repeat(np.exp2(rng.integers(-cols, cols + 1, shape[:-2] + (1, shape[-1] // 4))) * (rng.random(shape[:-2] + (1, shape[-1] // 4)) > 0.0625), 4, axis=-1).astype(np.float32)
    return mx_ref.flush(v.astype(BF))
T, CAPP = 256, 48
def even(n):
    return [T // n + (k < T % n) for k in range(n)]
def counts(rng, h, moves=10 * N * N):
    n = np.array([[h[(d - s) % N] for d in range(N)] for s in range(N)])[rng.permutation(N)][:, rng.permutation(N)]
    top = np.where(n > 0, CAPP, 0)
    for _ in range(moves):
        a, b = rng.permutation(N)[:2]; c, e = rng.permutation(N)[:2]
        k = rng.integers(0, min(n[a, e], n[b, c], top[a, c] - n[a, c], top[b, e] - n[b, e]) + 1)
        n[a, c] += k; n[b, e] += k; n[a, e] -= k; n[b, c] -= k
    return n
def lists(rng, n, back=False):
    a = np.full((N, N, CAPP), -1)
    for s in range(N):
        p = np.arange(T)[::-1] if back else rng.permutation(T)
        for d in range(N):
            k = rng.permutation(CAPP)[:n[s, d]]
            if back: k = np.sort(k)
            a[s, d, k] = p[:n[s, d]]; p = p[n[s, d]:]
    m = []
    for d in range(N):
        k = np.flatnonzero(a[:, d].reshape(-1) >= 0)
        m.append(table(k[::-1] if back else rng.permutation(k)))
    return {"send": np.stack([table(a[s].reshape(-1)) for s in range(N)]), "mine": np.stack(m), "prev": np.stack([m[(r - 1) % N] for r in range(N)])}
def setup_inputs(rng):
    return {"x": f(rng, N, 128, 4 * T), **lists(rng, counts(rng, even(N)))}
def setup_inputs_empty(rng):
    return {**setup_inputs(rng), **lists(rng, counts(rng, even(N - 1) + [0]))}
def setup_inputs_full(rng):
    return {**setup_inputs(rng), **lists(rng, counts(rng, [min(CAPP, max(0, T - k * CAPP)) for k in range(N)], 0))}
def setup_inputs_reversed(rng):
    return {**setup_inputs(rng), **lists(rng, counts(rng, even(N)), back=True)}
def setup_inputs_spread(rng):
    d = setup_inputs(rng); d["x"] = wide(rng, N, 128, 4 * T, cols=8); return d
def check_inputs(d):
    b = []
    v = np.abs(np.asarray(d["x"]).astype(np.float32))
    if not ((v == 0) | ((v >= 2.0 ** -30) & (v <= 2.0 ** 30))).all(): b.append("x")
    for r in range(N):
        c, m = entries(d["send"][r]), entries(d["mine"][r])
        if c.min() < -1 or not np.array_equal(np.sort(c[c >= 0]), np.arange(T)): b.append("send")
        arrived = np.concatenate([entries(d["send"][s])[r * CAPP:(r + 1) * CAPP] for s in range(N)])
        if not np.array_equal(np.sort(m), np.flatnonzero(arrived >= 0)): b.append("mine")
        if not np.array_equal(d["prev"][r], d["mine"][(r - 1) % N]): b.append("prev")
    return b
def reference(x, send, mine, prev):
    K = []
    for r in range(N):
        arrived = np.concatenate([cols(x[s], entries(send[s])[r * CAPP:(r + 1) * CAPP]) for s in range(N)], axis=1)
        K.append(cols(arrived, entries(mine[r])))
    Q = [mx_ref.quantize(t) for t in K]
    y = np.zeros((N, T, 2 * T), np.float32)
    for r in range(N):
        for p in range(T // 128):
            W = mx_ref.quantize(np.ascontiguousarray(K[r][:, 512 * p:512 * p + 512]))
            y[r, 128 * p:128 * p + 128, :T] = mx_ref.matmul(W, Q[r])
            y[r, 128 * p:128 * p + 128, T:] = mx_ref.matmul(W, Q[(r - 1) % N])
    return {"y": y}

@@ -1,0 +1,278 @@
+from concourse.bass import DstId, RemoteDMATransfer, IndirectOffsetOnAxis
+from concourse.mybir import dt, AluOpType, AxisListType, ActivationFunctionType
+
+N, NT, CAPP = 8, 256, 48
+ARR = N * CAPP
+NBUCK = (1, 2, 5)
+WIDTH = (128, 128, 240)
+W16 = CAPP // 16
+L16 = NT // 16
+NTILE = ARR // 128
+SKIP = 1000.0
+
+SCRATCH = {
+    "xs": ("sbuf", [128, 4 * NT], "bfloat16"),
+    "lsend": ("sbuf", [128, N * W16], "int32"),
+    "lists": ("sbuf", [128, 2 * L16], "int32"),
+    "wrap": ("sbuf", [128, 2 * L16], "int32"),
+    "turn": ("sbuf", [128, 2 * L16], "int32"),
+    "moff": ("sbuf", [128, 2 * L16], "uint16"),
+    "own_c": ("sbuf", [128, ARR], "float8_e4m3fn_x4"),
+    "own_s": ("sbuf", [128, ARR], "uint8"),
+    "prv_c": ("sbuf", [128, ARR], "float8_e4m3fn_x4"),
+    "prv_s": ("sbuf", [128, ARR], "uint8"),
+    "places": ("sbuf", [128, NT], "float32"),
+    "pcol": ("sbuf", [128, 4], "float32"),
+    "diag": ("sbuf", [128, 128], "float32"),
+    "inv": ("sbuf", [128, ARR], "float32"),
+    "pick": ("sbuf", [128, ARR], "float32"),
+    "idxf": ("sbuf", [128, 4], "float32"),
+    "idx": ("sbuf", [128, 4], "int32"),
+    "ps": ("psum", [128, 512 * (2 * NTILE + 1)], "float32"),
+}
+SEMAPHORES = ["ld_send", "ld_x", "ld_lists", "ld_g", "iot", "inv0", "zero", "selfc", "hand_c", "hand_s", "own_in",
+              "prv_in", "sent", "wr", "tu", "mo", "invd", "dia", "pk", "ixf", "ix", "pepx"]
+for _t in range(3):
+    SCRATCH["off%d" % _t] = ("sbuf", [128, NBUCK[_t] * W16], "uint16")
+    SCRATCH["h%d" % _t] = ("sbuf", [128, 4 * WIDTH[_t]], "bfloat16")
+    SCRATCH["q%d_c" % _t] = ("sbuf", [128, WIDTH[_t]], "float8_e4m3fn_x4")
+    SCRATCH["q%d_s" % _t] = ("sbuf", [128, WIDTH[_t]], "uint8")
+    SEMAPHORES += ["cv%d" % _t, "ga%d" % _t, "q%d" % _t]
+for _t in range(NTILE):
+    SCRATCH["raw%d" % _t] = ("sbuf", [128, 2 * ARR], "float32")
+    SCRATCH["row%d" % _t] = ("sbuf", [128, 2 * NT], "float32")
+    SEMAPHORES += ["peo%d" % _t, "pep%d" % _t, "evo%d" % _t, "evp%d" % _t, "rw%d" % _t, "st%d" % _t]
+
+
+def rank_program(g, core, T, topo):
+    rank = T.rank_of(core)
+    if rank is None:
+        return
+    V, S, Y, P, M = g.vector, g.scalar, g.sync, g.tensor, T.sem
+    COPY = ActivationFunctionType.Copy
+    cores = list(T.cores)
+    chip = [topo.chip(c) for c in cores]
+    shared = [d for d in range(N) if chip[d] == chip[(d + 1) % N]]
+    rest = [d for d in range(N) if d not in shared]
+    before = (rank - 1) % N
+
+    def head(r):
+        return r if r in shared else r - 1
+
+    def tiles(s):
+        a = sorted([d for d in shared if chip[d] != chip[s]], key=lambda d: (d - s) % N)
+        return a[:1], a[1:], [head(s)] + rest
+
+    def at(s, d):
+        for k, ds in enumerate(tiles(s)):
+            if d in ds:
+                return "q%d" % k, ds.index(d) * CAPP
+
+    def base(r):
+        return (head(r) + 2) % N
+
+    def slot(r, s):
+        return (s - base(r)) % N * CAPP
+
+    def plan(s):
+        away = [r for r in range(N) if chip[r] != chip[s]]
+        sib = [r for r in range(N) if r != s and chip[r] == chip[s]][0]
+        off = topo.engines(cores[s], cores[away[0]])
+        near = [e for e in topo.engines(cores[s], cores[sib]) if e not in off]
+        q = len(off) // 4
+        G = [off[q * k:q * k + q] for k in range(4)]
+
+        def deal(a, b, c, d):
+            return [G[c], G[d], G[a] + G[b]]
+
+        def move(r, d, buf, es, fs, sems=None):
+            return (r, es, fs, sems or (buf + "_in",) * 2) + at(s, d) + (buf, slot(r, s), CAPP)
+
+        hand = ("hand_c", "hand_s")
+        a0, a1, _ = tiles(s)
+        rounds = [[move(a0[0], a0[0], "own", off, off, hand)],
+                  [move(a1[0], a1[0], "own", G[0] + G[1], G[2] + G[3], hand),
+                   move(a1[1], a1[1], "own", G[2] + G[3], G[0] + G[1], hand)], [], [], [], []]
+        for k, step, buf, es, fs in ((2, 0, "own", deal(0, 1, 2, 3), deal(2, 3, 0, 1)),
+                                     (3, 1, "prv", deal(2, 3, 0, 1), deal(0, 1, 2, 3))):
+            for d in rest:
+                r = (d + step) % N
+                if r in away:
+                    rounds[k].append(move(r, d, buf, es.pop(0), fs.pop(0)))
+        w, h = len(near) // 4, len(near) // 2
+        pairs = ([(s, "prv"), (sib, "own")] if s in shared else [(sib, "own"), ((sib - 1) % N, "prv")])
+        for k, (d, buf) in enumerate(pairs):
+            rounds[4].append(move(sib, d, buf, near[k * w:k * w + w], near[h + k * w:h + k * w + w]))
+        if s in shared:
+            rounds[5].append((sib, near, near, ("prv_in",) * 2, "own", 0, "prv", 0, len(away) * CAPP))
+        return rounds
+
+    due = {}
+    for s in range(N):
+        for moves in plan(s):
+            for m in moves:
+                if m[0] == rank:
+                    for k in (0, 1):
+                        due[m[3][k]] = due.get(m[3][k], 0) + len(m[1 + k])
+    rounds = plan(rank)
+    sent = [0]
+
+    def bits(es):
+        m = 0
+        for e in es:
+            m |= 1 << e
+        return m
+
+    def issue(moves, kinds=(0, 1)):
+        for k in kinds:
+            ts = []
+            for m in moves:
+                dst, es, sem, (a, i, b, j, w) = m[0], m[1 + k], m[3][k], m[4:]
+                src, out = T[a + ("_c", "_s")[k]][:, i:i + w], T[b + ("_c", "_s")[k]][:, j:j + w]
+                if k == 0:
+                    src, out = src.bitcast(dt.uint8), out.bitcast(dt.uint8)
+                rid, pid = topo.addr(cores[dst])[:2]
+                ts.append(RemoteDMATransfer(dst_ids=[DstId(rid=rid, pnc=pid)], dma_engine_mask=bits(es),
+                                            remote_sem=M[sem], src=src, dst=out))
+                sent[0] += len(es)
+            g.remote_dma_fused(ts, local_sem=M.sent)
+
+    for k in range(5):
+        S.dma_start(T.lsend[16 * k:16 * k + 16, :], T.send[:]).then_inc(M.ld_send, 16)
+    for k in range(5, 8):
+        Y.dma_start(T.lsend[16 * k:16 * k + 16, :], T.send[:]).then_inc(M.ld_send, 16)
+    Y.dma_start(T.xs[:], T.x[:]).then_inc(M.ld_x, 16)
+    g.dma_start(T.lists[0:16, 0:L16], T.mine[:]).then_inc(M.ld_g, 16)
+    for k in range(1, 8):
+        Y.dma_start(T.lists[16 * k:16 * k + 16, 0:L16], T.mine[:]).then_inc(M.ld_lists, 16)
+    for k in range(8):
+        Y.dma_start(T.lists[16 * k:16 * k + 16, L16:2 * L16], T.prev[:]).then_inc(M.ld_lists, 16)
+    g.iota(T.places[:], [[1, NT]], 0, 0, allow_small_or_imprecise_dtypes=True).then_inc(M.iot, 1)
+    g.iota(T.pcol[:], [[0, 4]], 0, 1, allow_small_or_imprecise_dtypes=True).then_inc(M.iot, 1)
+    for k in (0, 1):
+        V.memset(T["h%d" % k][:, 4 * NBUCK[k] * CAPP:4 * WIDTH[k]], 0.0).then_inc(M.zero, 1)
+    V.memset(T.inv[:], SKIP).then_inc(M.inv0, 1)
+
+    V.wait_ge(M.ld_send, 128)
+    conv = [0, 0, 0]
+
+    def offsets(k, out, src):
+        V.tensor_scalar(out, src, 0, 4, AluOpType.max, AluOpType.mult).then_inc(M["cv%d" % k], 1)
+        conv[k] += 1
+
+    for k, ds in enumerate(tiles(rank)):
+        for i, d in enumerate(ds):
+            if d in shared:
+                offsets(k, T["off%d" % k][:, W16 * i:W16 * i + W16], T.lsend[:, W16 * d:W16 * d + W16])
+    for w in range(W16):
+        offsets(2, T.off2[:, W16 + w::W16], T.lsend[:, W16 * rest[0] + w::2 * W16])
+
+    def copy(eng, out, src, sem):
+        if eng is V:
+            V.tensor_copy(out, src).then_inc(sem, 1)
+        else:
+            S.activation(out, src, COPY).then_inc(sem, 1)
+
+    V.wait_ge(M.zero, 2)
+    V.wait_ge(M.ld_x, 16)
+    S.wait_ge(M.ld_x, 16)
+    for k in range(3):
+        n = 4 * NBUCK[k] * CAPP
+        for eng, ts in ((V, (0, 1)), (S, (2, 3))):
+            eng.wait_ge(M["cv%d" % k], conv[k])
+            for t in ts:
+                copy(eng, T["h%d" % k][:, t:n:4], T.xs[:, t:4 * NT].indirect(T["off%d" % k][:]), M["ga%d" % k])
+        V.wait_ge(M["ga%d" % k], 4)
+        V.quantize_mx(T["q%d_c" % k][:], T["q%d_s" % k][:], T["h%d" % k][:]).then_inc(M["q%d" % k], 1)
+
+    for k in range(3):
+        g.wait_ge(M["q%d" % k], 1)
+        issue(rounds[k])
+    issue(rounds[3])
+    issue(rounds[4])
+    for d, buf in ((rank, "own"), (before, "prv")):
+        q, i = at(rank, d)
+        j = slot(rank, rank)
+        Y.wait_ge(M[q], 1)
+        Y.dma_start(T[buf + "_c"][:, j:j + CAPP].bitcast(dt.uint8),
+                    T[q + "_c"][:, i:i + CAPP].bitcast(dt.uint8)).then_inc(M.selfc, 16)
+        Y.dma_start(T[buf + "_s"][:, j:j + CAPP], T[q + "_s"][:, i:i + CAPP]).then_inc(M.selfc, 16)
+    if rounds[5]:
+        for k, sem in enumerate(("hand_c", "hand_s")):
+            g.wait_ge(M[sem], due[sem])
+            issue(rounds[5], (k,))
+
+    b = base(rank) * CAPP
+    V.wait_ge(M.ld_lists, 240)
+    V.wait_ge(M.ld_g, 16)
+    V.tensor_scalar(T.wrap[:], T.lists[:], b, ARR, AluOpType.is_lt, AluOpType.mult).then_inc(M.wr, 1)
+    V.wait_ge(M.iot, 2)
+    V.tensor_scalar(T.diag[:], T.places[:, 0:128], T.pcol[:, 0:1], None, AluOpType.is_equal).then_inc(M.dia, 1)
+    V.wait_ge(M.wr, 1)
+    V.tensor_tensor(T.turn[:], T.lists[:], T.wrap[:], AluOpType.add).then_inc(M.tu, 1)
+    V.wait_ge(M.tu, 1)
+    V.tensor_scalar(T.moff[:], T.turn[:], b, None, AluOpType.subtract).then_inc(M.mo, 1)
+    V.wait_ge(M.mo, 1)
+    V.wait_ge(M.inv0, 1)
+    V.tensor_copy(T.inv[:].indirect(T.moff[:, 0:L16]), T.places[:]).then_inc(M.invd, 1)
+    V.wait_ge(M.invd, 1)
+    V.wait_ge(M.dia, 1)
+    for t in range(NTILE):
+        V.tensor_tensor(T.pick[:, 128 * t:128 * t + 128], T.inv[:, 128 * t:128 * t + 128], T.diag[:],
+                        AluOpType.mult).then_inc(M.pk, 1)
+    V.wait_ge(M.pk, NTILE)
+    for t in range(NTILE):
+        V.tensor_reduce(T.idxf[:, t:t + 1], T.pick[:, 128 * t:128 * t + 128], AxisListType.X,
+                        AluOpType.add).then_inc(M.ixf, 1)
+    V.wait_ge(M.ixf, NTILE)
+    V.tensor_copy(T.idx[:, 0:NTILE], T.idxf[:, 0:NTILE]).then_inc(M.ix, 1)
+
+    def product(t, side, a, b, k, sem):
+        P.matmul_mx(T.ps[:, 512 * k:512 * k + b - a], T.own_c[:, 128 * t:128 * t + 128],
+                    T.own_s[:, 128 * t:128 * t + 128], T[side + "_c"][:, a:b], T[side + "_s"][:, a:b],
+                    True, True).then_inc(sem, 1)
+
+    P.wait_ge(M.selfc, 64)
+    for sem in ("hand_c", "hand_s", "own_in"):
+        if sem in due:
+            P.wait_ge(M[sem], due[sem])
+    for t in range(NTILE):
+        product(t, "own", 0, ARR, t, M["peo%d" % t])
+    P.wait_ge(M.prv_in, due["prv_in"])
+    product(0, "prv", 0, ARR // 2, NTILE, M.pep0)
+    product(0, "prv", ARR // 2, ARR, 2 * NTILE, M.pepx)
+    for t in range(1, NTILE):
+        product(t, "prv", 0, ARR, NTILE + t, M["pep%d" % t])
+
+    def leave(eng, t, h, a, b, k, pe):
+        eng.wait_ge(pe, 1)
+        copy(eng, T["raw%d" % t][:, h * ARR + a:h * ARR + b], T.ps[:, 512 * k:512 * k + b - a],
+             M["ev%s%d" % ("op"[h], t)])
+
+    def order(eng, t, h, a, b, n):
+        eng.wait_ge(M["ev%s%d" % ("op"[h], t)], n)
+        win = T["raw%d" % t][:, h * ARR:h * ARR + ARR].indirect(T.moff[:, h * L16 + a // 16:h * L16 + b // 16])
+        copy(eng, T["row%d" % t][:, h * NT + a:h * NT + b], win, M["rw%d" % t])
+
+    S.wait_ge(M.mo, 1)
+    for eng, ts in ((V, (0, 2)), (S, (1,))):
+        for t in ts:
+            leave(eng, t, 0, 0, ARR, t, M["peo%d" % t])
+        for t in ts:
+            order(eng, t, 0, 0, NT, 1)
+    leave(V, 0, 1, 0, ARR // 2, NTILE, M.pep0)
+    leave(S, 0, 1, ARR // 2, ARR, 2 * NTILE, M.pepx)
+    order(V, 0, 1, 0, NT // 2, 2)
+    order(S, 0, 1, NT // 2, NT, 2)
+    for eng, t in ((S, 1), (V, 2)):
+        leave(eng, t, 1, 0, ARR, NTILE + t, M["pep%d" % t])
+        order(eng, t, 1, 0, NT, 1)
+
+    g.wait_ge(M.ix, 1)
+    for t in range(NTILE):
+        g.wait_ge(M["rw%d" % t], 2 if t else 3)
+        g.indirect_dma_start(T.y[:], IndirectOffsetOnAxis(ap=T.idx[:, t:t + 1], axis=0), T["row%d" % t][:], None,
+                             bounds_check=NT - 1, oob_is_err=False).then_inc(M["st%d" % t], 16)
+    g.wait_ge(M.sent, sent[0])
+    for t in range(NTILE):
+        g.wait_ge(M["st%d" % t], 16)

@@ -3,12 +3,13 @@ from concourse.mybir import dt, AluOpType, AxisListType, ActivationFunctionType
 
 N, NT, CAPP = 8, 256, 48
 ARR = N * CAPP
-NBUCK = (1, 2, 5)
-WIDTH = (128, 128, 240)
 W16 = CAPP // 16
 L16 = NT // 16
 NTILE = ARR // 128
 SKIP = 1000.0
+OWN, MID, PRV = 0, ARR - CAPP, ARR + CAPP
+NBUCK = (2, 3, 3)
+WIDTH = (128, 144, 144)
 
 SCRATCH = {
     "xs": ("sbuf", [128, 4 * NT], "bfloat16"),
@@ -17,10 +18,8 @@ SCRATCH = {
     "wrap": ("sbuf", [128, 2 * L16], "int32"),
     "turn": ("sbuf", [128, 2 * L16], "int32"),
     "moff": ("sbuf", [128, 2 * L16], "uint16"),
-    "own_c": ("sbuf", [128, ARR], "float8_e4m3fn_x4"),
-    "own_s": ("sbuf", [128, ARR], "uint8"),
-    "prv_c": ("sbuf", [128, ARR], "float8_e4m3fn_x4"),
-    "prv_s": ("sbuf", [128, ARR], "uint8"),
+    "u_c": ("sbuf", [128, PRV + ARR], "float8_e4m3fn_x4"),
+    "u_s": ("sbuf", [128, PRV + ARR], "uint8"),
     "places": ("sbuf", [128, NT], "float32"),
     "pcol": ("sbuf", [128, 4], "float32"),
     "diag": ("sbuf", [128, 128], "float32"),
@@ -30,14 +29,15 @@ SCRATCH = {
     "idx": ("sbuf", [128, 4], "int32"),
     "ps": ("psum", [128, 512 * (2 * NTILE + 1)], "float32"),
 }
-SEMAPHORES = ["ld_send", "ld_x", "ld_lists", "ld_g", "iot", "inv0", "zero", "selfc", "hand_c", "hand_s", "own_in",
-              "prv_in", "sent", "wr", "tu", "mo", "invd", "dia", "pk", "ixf", "ix", "pepx"]
+SEMAPHORES = ["ld_send", "ld_x", "ld_lists", "ld_g", "iot", "inv0", "zero", "hand_c", "hand_s", "rel_c", "rel_s",
+              "own_in", "prv_in", "sent", "wr", "tu", "mo", "invd", "dia", "pk", "ixf", "ix", "pepx"]
 for _t in range(3):
-    SCRATCH["off%d" % _t] = ("sbuf", [128, NBUCK[_t] * W16], "uint16")
+    SCRATCH["off%d" % _t] = ("sbuf", [128, 2 * ((NBUCK[_t] * W16 + 1) // 2)], "uint16")
     SCRATCH["h%d" % _t] = ("sbuf", [128, 4 * WIDTH[_t]], "bfloat16")
+    SEMAPHORES += ["cv%d" % _t, "ga%d" % _t, "q%d" % _t]
+for _t in range(2):
     SCRATCH["q%d_c" % _t] = ("sbuf", [128, WIDTH[_t]], "float8_e4m3fn_x4")
     SCRATCH["q%d_s" % _t] = ("sbuf", [128, WIDTH[_t]], "uint8")
-    SEMAPHORES += ["cv%d" % _t, "ga%d" % _t, "q%d" % _t]
 for _t in range(NTILE):
     SCRATCH["raw%d" % _t] = ("sbuf", [128, 2 * ARR], "float32")
     SCRATCH["row%d" % _t] = ("sbuf", [128, 2 * NT], "float32")
@@ -45,76 +45,89 @@ for _t in range(NTILE):
 
 
 def rank_program(g, core, T, topo):
-    rank = T.rank_of(core)
-    if rank is None:
-        return
     V, S, Y, P, M = g.vector, g.scalar, g.sync, g.tensor, T.sem
     COPY = ActivationFunctionType.Copy
     cores = list(T.cores)
     chip = [topo.chip(c) for c in cores]
     shared = [d for d in range(N) if chip[d] == chip[(d + 1) % N]]
-    rest = [d for d in range(N) if d not in shared]
-    before = (rank - 1) % N
 
     def head(r):
         return r if r in shared else r - 1
 
+    def wants(d):
+        return [(d, OWN, "own_in"), ((d + 1) % N, PRV, "prv_in")]
+
     def tiles(s):
-        a = sorted([d for d in shared if chip[d] != chip[s]], key=lambda d: (d - s) % N)
-        return a[:1], a[1:], [head(s)] + rest
+        far = [d for d in range(N) if all(chip[r] != chip[s] for r, _, _ in wants(d))]
+        far.sort(key=lambda d: (d - s) % N)
+        ends = [s, (s - 1) % N]
+        return ([d for d in far if d not in shared], [d for d in far if d in shared],
+                [s] + [d for d in range(N) if d not in far + ends] + ends[1:])
 
     def at(s, d):
         for k, ds in enumerate(tiles(s)):
             if d in ds:
-                return "q%d" % k, ds.index(d) * CAPP
+                return (("q0", "q1", "u")[k], ds.index(d) * CAPP + (MID if k == 2 else 0))
 
-    def base(r):
-        return (head(r) + 2) % N
+    def slot(r, part, s):
+        return part + (s - r - (part == OWN)) % N * CAPP
 
-    def slot(r, s):
-        return (s - base(r)) % N * CAPP
+    def helpers(h):
+        return [c for c in topo.cores_of(cores[h])
+                if topo.die(c) != topo.die(cores[h]) and all(topo.may_write(c, r) for r in cores)]
 
-    def plan(s):
-        away = [r for r in range(N) if chip[r] != chip[s]]
-        sib = [r for r in range(N) if r != s and chip[r] == chip[s]][0]
-        off = topo.engines(cores[s], cores[away[0]])
+    def split(es, n):
+        return [es[k * len(es) // n:(k + 1) * len(es) // n] for k in range(n)]
+
+    def plan_rank(s):
+        h = head(s)
+        sib = 2 * h + 1 - s
+        ta, tb, tc = tiles(s)
+        off = topo.engines(cores[s], cores[tb[0]])
         near = [e for e in topo.engines(cores[s], cores[sib]) if e not in off]
-        q = len(off) // 4
-        G = [off[q * k:q * k + q] for k in range(4)]
+        G = split(off, 4)
+        deal = ([G[0] + G[1], G[2], G[3]], [G[2] + G[3], G[0], G[1]])
 
-        def deal(a, b, c, d):
-            return [G[c], G[d], G[a] + G[b]]
+        def relay(k):
+            return [(c, es, ("rel_c", "rel_s")[k]) + at(s, d) + ((s - h) * CAPP, CAPP)
+                    for d, c, es in zip(ta, helpers(h), split(near, 2))]
 
-        def move(r, d, buf, es, fs, sems=None):
-            return (r, es, fs, sems or (buf + "_in",) * 2) + at(s, d) + (buf, slot(r, s), CAPP)
+        def heads(k):
+            return [(cores[d], es, ("hand_c", "hand_s")[k]) + at(s, d) + (slot(d, OWN, s), CAPP)
+                    for d, es in zip(tb, deal[k])]
 
-        hand = ("hand_c", "hand_s")
-        a0, a1, _ = tiles(s)
-        rounds = [[move(a0[0], a0[0], "own", off, off, hand)],
-                  [move(a1[0], a1[0], "own", G[0] + G[1], G[2] + G[3], hand),
-                   move(a1[1], a1[1], "own", G[2] + G[3], G[0] + G[1], hand)], [], [], [], []]
-        for k, step, buf, es, fs in ((2, 0, "own", deal(0, 1, 2, 3), deal(2, 3, 0, 1)),
-                                     (3, 1, "prv", deal(2, 3, 0, 1), deal(0, 1, 2, 3))):
-            for d in rest:
-                r = (d + step) % N
-                if r in away:
-                    rounds[k].append(move(r, d, buf, es.pop(0), fs.pop(0)))
-        w, h = len(near) // 4, len(near) // 2
-        pairs = ([(s, "prv"), (sib, "own")] if s in shared else [(sib, "own"), ((sib - 1) % N, "prv")])
-        for k, (d, buf) in enumerate(pairs):
-            rounds[4].append(move(sib, d, buf, near[k * w:k * w + w], near[h + k * w:h + k * w + w]))
-        if s in shared:
-            rounds[5].append((sib, near, near, ("prv_in",) * 2, "own", 0, "prv", 0, len(away) * CAPP))
-        return rounds
+        far = [(r, d, part, sem) for d in tc for r, part, sem in wants(d) if chip[r] != chip[s]]
+        close = [(r, d, part, sem) for d in tc for r, part, sem in wants(d) if r == sib and not s == h == d]
+        last = [(cores[r], es, sem) + at(s, d) + (slot(r, part, s), CAPP)
+                for ms, pool in ((far, off), (close, near))
+                for (r, d, part, sem), es in zip(ms, split(pool, len(ms)))]
+        calls = [(["q0"], 0, relay(0)), (["q1"], 0, heads(0)), ([], 1, relay(1) + heads(1)),
+                 (["q2"], 0, last), ([], 1, last)]
+        if s == h:
+            for k, sem in enumerate(("hand_c", "hand_s")):
+                calls.append(([sem], k, [(cores[sib], near, "prv_in", "u", OWN + CAPP, PRV + CAPP, ARR - CAPP)]))
+        return calls
 
-    due = {}
-    for s in range(N):
-        for moves in plan(s):
+    def plan_helper(h, i):
+        d = tiles(h)[0][i]
+        c = helpers(h)[i]
+        es = split(topo.engines(c, cores[d]), 2)
+        return [([sem], k, [(cores[r], es[j], rs, "u", 0, slot(r, part, h), 2 * CAPP)
+                            for j, (r, part, rs) in enumerate(wants(d))])
+                for k, sem in enumerate(("rel_c", "rel_s"))]
+
+    plans = {cores[s]: plan_rank(s) for s in range(N)}
+    for h in shared:
+        for i in range(NBUCK[0]):
+            plans[helpers(h)[i]] = plan_helper(h, i)
+    if core not in plans:
+        return
+    due = {"q0": 1, "q1": 1, "q2": 1}
+    for calls in plans.values():
+        for _, _, moves in calls:
             for m in moves:
-                if m[0] == rank:
-                    for k in (0, 1):
-                        due[m[3][k]] = due.get(m[3][k], 0) + len(m[1 + k])
-    rounds = plan(rank)
+                if m[0] == core:
+                    due[m[2]] = due.get(m[2], 0) + len(m[1])
     sent = [0]
 
     def bits(es):
@@ -123,19 +136,26 @@ def rank_program(g, core, T, topo):
             m |= 1 << e
         return m
 
-    def issue(moves, kinds=(0, 1)):
-        for k in kinds:
+    def send_all():
+        for waits, k, moves in plans[core]:
+            for sem in waits:
+                g.wait_ge(M[sem], due[sem])
             ts = []
-            for m in moves:
-                dst, es, sem, (a, i, b, j, w) = m[0], m[1 + k], m[3][k], m[4:]
-                src, out = T[a + ("_c", "_s")[k]][:, i:i + w], T[b + ("_c", "_s")[k]][:, j:j + w]
+            for dst, es, sem, a, i, j, w in moves:
+                src, out = T[a + ("_c", "_s")[k]][:, i:i + w], T["u" + ("_c", "_s")[k]][:, j:j + w]
                 if k == 0:
                     src, out = src.bitcast(dt.uint8), out.bitcast(dt.uint8)
-                rid, pid = topo.addr(cores[dst])[:2]
+                rid, pid = topo.addr(dst)[:2]
                 ts.append(RemoteDMATransfer(dst_ids=[DstId(rid=rid, pnc=pid)], dma_engine_mask=bits(es),
                                             remote_sem=M[sem], src=src, dst=out))
                 sent[0] += len(es)
             g.remote_dma_fused(ts, local_sem=M.sent)
+
+    rank = T.rank_of(core)
+    if rank is None:
+        send_all()
+        g.wait_ge(M.sent, sent[0])
+        return
 
     for k in range(5):
         S.dma_start(T.lsend[16 * k:16 * k + 16, :], T.send[:]).then_inc(M.ld_send, 16)
@@ -149,23 +169,14 @@ def rank_program(g, core, T, topo):
         Y.dma_start(T.lists[16 * k:16 * k + 16, L16:2 * L16], T.prev[:]).then_inc(M.ld_lists, 16)
     g.iota(T.places[:], [[1, NT]], 0, 0, allow_small_or_imprecise_dtypes=True).then_inc(M.iot, 1)
     g.iota(T.pcol[:], [[0, 4]], 0, 1, allow_small_or_imprecise_dtypes=True).then_inc(M.iot, 1)
-    for k in (0, 1):
-        V.memset(T["h%d" % k][:, 4 * NBUCK[k] * CAPP:4 * WIDTH[k]], 0.0).then_inc(M.zero, 1)
+    V.memset(T.h0[:, 4 * NBUCK[0] * CAPP:4 * WIDTH[0]], 0.0).then_inc(M.zero, 1)
     V.memset(T.inv[:], SKIP).then_inc(M.inv0, 1)
 
     V.wait_ge(M.ld_send, 128)
-    conv = [0, 0, 0]
-
-    def offsets(k, out, src):
-        V.tensor_scalar(out, src, 0, 4, AluOpType.max, AluOpType.mult).then_inc(M["cv%d" % k], 1)
-        conv[k] += 1
-
     for k, ds in enumerate(tiles(rank)):
         for i, d in enumerate(ds):
-            if d in shared:
-                offsets(k, T["off%d" % k][:, W16 * i:W16 * i + W16], T.lsend[:, W16 * d:W16 * d + W16])
-    for w in range(W16):
-        offsets(2, T.off2[:, W16 + w::W16], T.lsend[:, W16 * rest[0] + w::2 * W16])
+            V.tensor_scalar(T["off%d" % k][:, W16 * i:W16 * i + W16], T.lsend[:, W16 * d:W16 * d + W16], 0, 4,
+                            AluOpType.max, AluOpType.mult).then_inc(M["cv%d" % k], 1)
 
     def copy(eng, out, src, sem):
         if eng is V:
@@ -173,46 +184,37 @@ def rank_program(g, core, T, topo):
         else:
             S.activation(out, src, COPY).then_inc(sem, 1)
 
-    V.wait_ge(M.zero, 2)
+    V.wait_ge(M.zero, 1)
     V.wait_ge(M.ld_x, 16)
     S.wait_ge(M.ld_x, 16)
     for k in range(3):
-        n = 4 * NBUCK[k] * CAPP
+        n = NBUCK[k] * CAPP
         for eng, ts in ((V, (0, 1)), (S, (2, 3))):
-            eng.wait_ge(M["cv%d" % k], conv[k])
+            eng.wait_ge(M["cv%d" % k], NBUCK[k])
             for t in ts:
-                copy(eng, T["h%d" % k][:, t:n:4], T.xs[:, t:4 * NT].indirect(T["off%d" % k][:]), M["ga%d" % k])
+                copy(eng, T["h%d" % k][:, t:4 * n:4],
+                     T.xs[:, t:4 * NT].indirect(T["off%d" % k][:, 0:NBUCK[k] * W16]), M["ga%d" % k])
         V.wait_ge(M["ga%d" % k], 4)
-        V.quantize_mx(T["q%d_c" % k][:], T["q%d_s" % k][:], T["h%d" % k][:]).then_inc(M["q%d" % k], 1)
+        q, a = (("q0", 0), ("q1", 0), ("u", MID))[k]
+        V.quantize_mx(T[q + "_c"][:, a:a + WIDTH[k]], T[q + "_s"][:, a:a + WIDTH[k]],
+                      T["h%d" % k][:]).then_inc(M["q%d" % k], 1)
 
-    for k in range(3):
-        g.wait_ge(M["q%d" % k], 1)
-        issue(rounds[k])
-    issue(rounds[3])
-    issue(rounds[4])
-    for d, buf in ((rank, "own"), (before, "prv")):
-        q, i = at(rank, d)
-        j = slot(rank, rank)
-        Y.wait_ge(M[q], 1)
-        Y.dma_start(T[buf + "_c"][:, j:j + CAPP].bitcast(dt.uint8),
-                    T[q + "_c"][:, i:i + CAPP].bitcast(dt.uint8)).then_inc(M.selfc, 16)
-        Y.dma_start(T[buf + "_s"][:, j:j + CAPP], T[q + "_s"][:, i:i + CAPP]).then_inc(M.selfc, 16)
-    if rounds[5]:
-        for k, sem in enumerate(("hand_c", "hand_s")):
-            g.wait_ge(M[sem], due[sem])
-            issue(rounds[5], (k,))
+    send_all()
 
-    b = base(rank) * CAPP
     V.wait_ge(M.ld_lists, 240)
     V.wait_ge(M.ld_g, 16)
-    V.tensor_scalar(T.wrap[:], T.lists[:], b, ARR, AluOpType.is_lt, AluOpType.mult).then_inc(M.wr, 1)
+    base = [(rank + 1) % N * CAPP, rank * CAPP]
+    half = [slice(0, L16), slice(L16, 2 * L16)]
+    for b, c in zip(base, half):
+        V.tensor_scalar(T.wrap[:, c], T.lists[:, c], b, ARR, AluOpType.is_lt, AluOpType.mult).then_inc(M.wr, 1)
     V.wait_ge(M.iot, 2)
     V.tensor_scalar(T.diag[:], T.places[:, 0:128], T.pcol[:, 0:1], None, AluOpType.is_equal).then_inc(M.dia, 1)
-    V.wait_ge(M.wr, 1)
+    V.wait_ge(M.wr, 2)
     V.tensor_tensor(T.turn[:], T.lists[:], T.wrap[:], AluOpType.add).then_inc(M.tu, 1)
     V.wait_ge(M.tu, 1)
-    V.tensor_scalar(T.moff[:], T.turn[:], b, None, AluOpType.subtract).then_inc(M.mo, 1)
-    V.wait_ge(M.mo, 1)
+    for b, c in zip(base, half):
+        V.tensor_scalar(T.moff[:, c], T.turn[:, c], b, None, AluOpType.subtract).then_inc(M.mo, 1)
+    V.wait_ge(M.mo, 2)
     V.wait_ge(M.inv0, 1)
     V.tensor_copy(T.inv[:].indirect(T.moff[:, 0:L16]), T.places[:]).then_inc(M.invd, 1)
     V.wait_ge(M.invd, 1)
@@ -227,22 +229,10 @@ def rank_program(g, core, T, topo):
     V.wait_ge(M.ixf, NTILE)
     V.tensor_copy(T.idx[:, 0:NTILE], T.idxf[:, 0:NTILE]).then_inc(M.ix, 1)
 
-    def product(t, side, a, b, k, sem):
-        P.matmul_mx(T.ps[:, 512 * k:512 * k + b - a], T.own_c[:, 128 * t:128 * t + 128],
-                    T.own_s[:, 128 * t:128 * t + 128], T[side + "_c"][:, a:b], T[side + "_s"][:, a:b],
+    def product(t, part, a, b, k, sem):
+        P.matmul_mx(T.ps[:, 512 * k:512 * k + b - a], T.u_c[:, 128 * t:128 * t + 128],
+                    T.u_s[:, 128 * t:128 * t + 128], T.u_c[:, part + a:part + b], T.u_s[:, part + a:part + b],
                     True, True).then_inc(sem, 1)
-
-    P.wait_ge(M.selfc, 64)
-    for sem in ("hand_c", "hand_s", "own_in"):
-        if sem in due:
-            P.wait_ge(M[sem], due[sem])
-    for t in range(NTILE):
-        product(t, "own", 0, ARR, t, M["peo%d" % t])
-    P.wait_ge(M.prv_in, due["prv_in"])
-    product(0, "prv", 0, ARR // 2, NTILE, M.pep0)
-    product(0, "prv", ARR // 2, ARR, 2 * NTILE, M.pepx)
-    for t in range(1, NTILE):
-        product(t, "prv", 0, ARR, NTILE + t, M["pep%d" % t])
 
     def leave(eng, t, h, a, b, k, pe):
         eng.wait_ge(pe, 1)
@@ -254,23 +244,47 @@ def rank_program(g, core, T, topo):
         win = T["raw%d" % t][:, h * ARR:h * ARR + ARR].indirect(T.moff[:, h * L16 + a // 16:h * L16 + b // 16])
         copy(eng, T["row%d" % t][:, h * NT + a:h * NT + b], win, M["rw%d" % t])
 
-    S.wait_ge(M.mo, 1)
-    for eng, ts in ((V, (0, 2)), (S, (1,))):
-        for t in ts:
-            leave(eng, t, 0, 0, ARR, t, M["peo%d" % t])
-        for t in ts:
-            order(eng, t, 0, 0, NT, 1)
-    leave(V, 0, 1, 0, ARR // 2, NTILE, M.pep0)
-    leave(S, 0, 1, ARR // 2, ARR, 2 * NTILE, M.pepx)
-    order(V, 0, 1, 0, NT // 2, 2)
-    order(S, 0, 1, NT // 2, NT, 2)
-    for eng, t in ((S, 1), (V, 2)):
-        leave(eng, t, 1, 0, ARR, NTILE + t, M["pep%d" % t])
-        order(eng, t, 1, 0, NT, 1)
+    P.wait_ge(M.q2, 1)
+    for sem in ("hand_c", "hand_s", "own_in"):
+        if sem in due:
+            P.wait_ge(M[sem], due[sem])
+    S.wait_ge(M.mo, 2)
+    if rank in shared:
+        for t in range(NTILE):
+            product(t, OWN, 0, ARR, t, M["peo%d" % t])
+        P.wait_ge(M.prv_in, due["prv_in"])
+        product(0, PRV, 0, ARR // 2, NTILE, M.pep0)
+        product(0, PRV, ARR // 2, ARR, 2 * NTILE, M.pepx)
+        for t in range(1, NTILE):
+            product(t, PRV, 0, ARR, NTILE + t, M["pep%d" % t])
+        for eng, ts in ((V, (0, 2)), (S, (1,))):
+            for t in ts:
+                leave(eng, t, 0, 0, ARR, t, M["peo%d" % t])
+            for t in ts:
+                order(eng, t, 0, 0, NT, 1)
+        leave(V, 0, 1, 0, ARR // 2, NTILE, M.pep0)
+        leave(S, 0, 1, ARR // 2, ARR, 2 * NTILE, M.pepx)
+        order(V, 0, 1, 0, NT // 2, 2)
+        order(S, 0, 1, NT // 2, NT, 2)
+        for eng, t in ((S, 1), (V, 2)):
+            leave(eng, t, 1, 0, ARR, NTILE + t, M["pep%d" % t])
+            order(eng, t, 1, 0, NT, 1)
+        pieces = [3, 2, 2]
+    else:
+        for t in range(NTILE):
+            product(t, OWN, 0, ARR, t, M["peo%d" % t])
+            if t == 0:
+                P.wait_ge(M.prv_in, due["prv_in"])
+            product(t, PRV, 0, ARR, NTILE + t, M["pep%d" % t])
+        for t in range(NTILE):
+            for eng, h in ((V, 0), (S, 1)):
+                leave(eng, t, h, 0, ARR, h * NTILE + t, M["pe%s%d" % ("op"[h], t)])
+                order(eng, t, h, 0, NT, 1)
+        pieces = [2, 2, 2]
 
     g.wait_ge(M.ix, 1)
     for t in range(NTILE):
-        g.wait_ge(M["rw%d" % t], 2 if t else 3)
+        g.wait_ge(M["rw%d" % t], pieces[t])
         g.indirect_dma_start(T.y[:], IndirectOffsetOnAxis(ap=T.idx[:, t:t + 1], axis=0), T["row%d" % t][:], None,
                              bounds_check=NT - 1, oob_is_err=False).then_inc(M["st%d" % t], 16)
     g.wait_ge(M.sent, sent[0])

@@ -7,30 +7,34 @@ W16 = CAPP // 16
 L16 = NT // 16
 NTILE = ARR // 128
 SKIP = 1000.0
-OWN, MID, PRV = 0, ARR - CAPP, ARR + CAPP
+LOW, MID, HIGH = 0, ARR - CAPP, ARR + CAPP
 NBUCK = (2, 3, 3)
 WIDTH = (128, 144, 144)
+PAD = WIDTH[0] - NBUCK[0] * CAPP
 
 SCRATCH = {
     "xs": ("sbuf", [128, 4 * NT], "bfloat16"),
     "lsend": ("sbuf", [128, N * W16], "int32"),
     "lists": ("sbuf", [128, 2 * L16], "int32"),
-    "wrap": ("sbuf", [128, 2 * L16], "int32"),
-    "turn": ("sbuf", [128, 2 * L16], "int32"),
+    "terms": ("sbuf", [128, 4 * N * L16], "int32"),
     "moff": ("sbuf", [128, 2 * L16], "uint16"),
-    "u_c": ("sbuf", [128, PRV + ARR], "float8_e4m3fn_x4"),
-    "u_s": ("sbuf", [128, PRV + ARR], "uint8"),
+    "u_c": ("sbuf", [128, HIGH + ARR], "float8_e4m3fn_x4"),
+    "u_s": ("sbuf", [128, HIGH + ARR], "uint8"),
     "places": ("sbuf", [128, NT], "float32"),
-    "pcol": ("sbuf", [128, 4], "float32"),
-    "diag": ("sbuf", [128, 128], "float32"),
+    "rown": ("sbuf", [128, 4], "int32"),
+    "roff": ("sbuf", [128, 4], "uint16"),
+    "skew": ("sbuf", [128, 16 * NTILE], "int32"),
+    "low": ("sbuf", [128, 16 * NTILE], "int32"),
+    "diag": ("sbuf", [128, 16 * NTILE], "float32"),
     "inv": ("sbuf", [128, ARR], "float32"),
-    "pick": ("sbuf", [128, ARR], "float32"),
+    "pick": ("sbuf", [128, 16 * NTILE], "float32"),
     "idxf": ("sbuf", [128, 4], "float32"),
     "idx": ("sbuf", [128, 4], "int32"),
-    "ps": ("psum", [128, 512 * (2 * NTILE + 1)], "float32"),
+    "ps": ("psum", [128, 512 * 8], "float32"),
 }
-SEMAPHORES = ["ld_send", "ld_x", "ld_lists", "ld_g", "iot", "inv0", "zero", "hand_c", "hand_s", "rel_c", "rel_s",
-              "own_in", "prv_in", "sent", "wr", "tu", "mo", "invd", "dia", "pk", "ixf", "ix", "pepx"]
+SEMAPHORES = ["ld_send", "ld_x", "ld_lists", "ld_g", "cst", "iot", "one", "inv0", "zero", "hand_c", "hand_s",
+              "rel_c", "rel_s", "join_s", "sib_c", "sib_s", "low_in", "high0", "high1", "high2", "sent", "tm", "mo", "invd", "pk",
+              "ixf", "ix"]
 for _t in range(3):
     SCRATCH["off%d" % _t] = ("sbuf", [128, 2 * ((NBUCK[_t] * W16 + 1) // 2)], "uint16")
     SCRATCH["h%d" % _t] = ("sbuf", [128, 4 * WIDTH[_t]], "bfloat16")
@@ -41,7 +45,8 @@ for _t in range(2):
 for _t in range(NTILE):
     SCRATCH["raw%d" % _t] = ("sbuf", [128, 2 * ARR], "float32")
     SCRATCH["row%d" % _t] = ("sbuf", [128, 2 * NT], "float32")
-    SEMAPHORES += ["peo%d" % _t, "pep%d" % _t, "evo%d" % _t, "evp%d" % _t, "rw%d" % _t, "st%d" % _t]
+    SEMAPHORES += ["ev%d0" % _t, "ev%d1" % _t, "rw%d" % _t, "st%d" % _t]
+SEMAPHORES += ["pe%d" % _t for _t in range(9)]
 
 
 def rank_program(g, core, T, topo):
@@ -54,72 +59,117 @@ def rank_program(g, core, T, topo):
     def head(r):
         return r if r in shared else r - 1
 
+    def sib(r):
+        return 2 * head(r) + 1 - r
+
     def wants(d):
-        return [(d, OWN, "own_in"), ((d + 1) % N, PRV, "prv_in")]
+        return [d, (d + 1) % N]
+
+    def part(d):
+        return LOW if d in shared else HIGH
 
     def tiles(s):
-        far = [d for d in range(N) if all(chip[r] != chip[s] for r, _, _ in wants(d))]
+        far = [d for d in range(N) if all(chip[r] != chip[s] for r in wants(d))]
         far.sort(key=lambda d: (d - s) % N)
-        ends = [s, (s - 1) % N]
+        ends = sorted([s, (s - 1) % N], key=part)
         return ([d for d in far if d not in shared], [d for d in far if d in shared],
-                [s] + [d for d in range(N) if d not in far + ends] + ends[1:])
+                ends[:1] + [d for d in range(N) if d not in far + ends] + ends[1:])
 
     def at(s, d):
         for k, ds in enumerate(tiles(s)):
             if d in ds:
-                return (("q0", "q1", "u")[k], ds.index(d) * CAPP + (MID if k == 2 else 0))
-
-    def slot(r, part, s):
-        return part + (s - r - (part == OWN)) % N * CAPP
+                return (("q0", "q1", "u")[k], ds.index(d) * CAPP + (PAD, 0, MID)[k])
 
     def helpers(h):
         return [c for c in topo.cores_of(cores[h])
                 if topo.die(c) != topo.die(cores[h]) and all(topo.may_write(c, r) for r in cores)]
 
+    def road(h, d, r):
+        if d not in tiles(h)[0]:
+            return "joined"
+        return "direct" if r == d and topo.same_plane(chip[h], chip[r]) else "helper%d" % tiles(h)[0].index(d)
+
+    def relays(h, k):
+        return [(c, d, [r for r in wants(d) if road(h, d, r) != "direct"]) for d, c in zip(tiles(h)[0], helpers(h))]
+
+    def senders(r, d):
+        if d in shared:
+            return [(r + 1 + k) % N for k in range(N)]
+        out = [r, sib(r)]
+        for way in ("direct", "helper1", "joined", "helper0"):
+            for h in shared:
+                if h != head(r) and road(h, d, r) == way:
+                    out += pair(h, d)
+        return out
+
+    def pair(h, d):
+        return [h, h + 1] if d in (tiles(h)[0][1], tiles(h)[2][2]) else [h + 1, h]
+
+    def slot(r, d, s):
+        return part(d) + senders(r, d).index(s) * CAPP
+
+    def high(r, d, s):
+        return "high%d" % ((slot(r, d, s) - HIGH) // 128)
+
+    def joined(h):
+        runs = [(d, r) for d in tiles(h)[2] if d not in shared for r in wants(d) if chip[r] != chip[h]]
+        return [(d, r, min(slot(r, d, h), slot(r, d, h + 1)), 2 * CAPP * (i + 1)) for i, (d, r) in enumerate(runs)]
+
     def split(es, n):
         return [es[k * len(es) // n:(k + 1) * len(es) // n] for k in range(n)]
 
     def plan_rank(s):
-        h = head(s)
-        sib = 2 * h + 1 - s
+        h, o = head(s), sib(s)
         ta, tb, tc = tiles(s)
         off = topo.engines(cores[s], cores[tb[0]])
-        near = [e for e in topo.engines(cores[s], cores[sib]) if e not in off]
+        near = [e for e in topo.engines(cores[s], cores[o]) if e not in off]
         G = split(off, 4)
         deal = ([G[0] + G[1], G[2], G[3]], [G[2] + G[3], G[0], G[1]])
 
         def relay(k):
-            return [(c, es, ("rel_c", "rel_s")[k]) + at(s, d) + ((s - h) * CAPP, CAPP)
-                    for d, c, es in zip(ta, helpers(h), split(near, 2))]
+            return [(c, es, ("rel_c", "rel_s")[k]) + at(s, d) + (pair(h, d).index(s) * CAPP, CAPP)
+                    for (c, d, _), es in zip(relays(h, k), split(near, 2) if k else (off, near))]
+
+        def direct(k):
+            return [(cores[d], off, high(d, d, s)) + at(s, d) + (slot(d, d, s), CAPP)
+                    for d in ta if road(h, d, d) == "direct" and (k == 0 or s == h)]
 
         def heads(k):
-            return [(cores[d], es, ("hand_c", "hand_s")[k]) + at(s, d) + (slot(d, OWN, s), CAPP)
+            return [(cores[d], es, ("hand_c", "hand_s")[k]) + at(s, d) + (slot(d, d, s), CAPP)
                     for d, es in zip(tb, deal[k])]
 
-        far = [(r, d, part, sem) for d in tc for r, part, sem in wants(d) if chip[r] != chip[s]]
-        close = [(r, d, part, sem) for d in tc for r, part, sem in wants(d) if r == sib and not s == h == d]
-        last = [(cores[r], es, sem) + at(s, d) + (slot(r, part, s), CAPP)
-                for ms, pool in ((far, off), (close, near))
-                for (r, d, part, sem), es in zip(ms, split(pool, len(ms)))]
-        calls = [(["q0"], 0, relay(0)), (["q1"], 0, heads(0)), ([], 1, relay(1) + heads(1)),
-                 (["q2"], 0, last), ([], 1, last)]
-        if s == h:
-            for k, sem in enumerate(("hand_c", "hand_s")):
-                calls.append(([sem], k, [(cores[sib], near, "prv_in", "u", OWN + CAPP, PRV + CAPP, ARR - CAPP)]))
-        return calls
+        def last(k):
+            close = [d for d in tc if o in wants(d)]
+            pool = split(near, 2)[0] if k else near
+            return ([(cores[o], es, "low_in" if d in shared else ("sib_c", "sib_s")[k]) + at(s, d)
+                     + (slot(o, d, s), CAPP) for d, es in zip(close, split(pool, len(close)))] +
+                    [(helpers(h)[1], es, "join_s") + at(s, d) + (at_helper + slot(r, d, s) - first, CAPP)
+                     for (d, r, first, at_helper), es in zip([j for j in joined(h) if j[0] == j[1]], split(near, 2)[1:])
+                     if k])
 
-    def plan_helper(h, i):
-        d = tiles(h)[0][i]
-        c = helpers(h)[i]
-        es = split(topo.engines(c, cores[d]), 2)
-        return [([sem], k, [(cores[r], es[j], rs, "u", 0, slot(r, part, h), 2 * CAPP)
-                            for j, (r, part, rs) in enumerate(wants(d))])
-                for k, sem in enumerate(("rel_c", "rel_s"))]
+        calls = [(["q0"], 0, relay(0)), (["q1"], 0, heads(0)), ([], 1, heads(1) + relay(1)),
+                 (["q2"], 0, direct(0) + last(0)), ([], 1, direct(1) + last(1))]
+        for d, r, first, _ in joined(h):
+            if d == tc[2]:
+                for k in range(1 + (d != r)):
+                    calls.append(([("sib_c", "sib_s")[k]], k,
+                                  [(cores[r], off, high(r, d, s), "u", HIGH, first, 2 * CAPP)]))
+        for k in range(2 * (s == h)):
+            calls.append(([("hand_c", "hand_s")[k]], k,
+                          [(cores[o], near, "low_in", "u", LOW + CAPP, LOW, ARR - 2 * CAPP)]))
+        return calls
 
     plans = {cores[s]: plan_rank(s) for s in range(N)}
     for h in shared:
-        for i in range(NBUCK[0]):
-            plans[helpers(h)[i]] = plan_helper(h, i)
+        for k, sem in enumerate(("rel_c", "rel_s")):
+            for c, d, rs in relays(h, k):
+                s, es = pair(h, d)[0], topo.engines(c, cores[rs[0]])
+                plans.setdefault(c, []).append(([sem], k, [
+                    (cores[r], e, high(r, d, s), "u", 0, slot(r, d, s), 2 * CAPP)
+                    for r, e in zip(rs, split(es, len(rs)))]))
+        plans[c].append(([], 1, [(cores[d], es, high(d, d, h + 1), "u", CAPP, slot(d, d, h + 1), CAPP)]))
+        plans[helpers(h)[1]].append((["join_s"], 1, [(cores[r], es, "high%d" % ((first - HIGH) // 128), "u", i, first,
+                                                      2 * CAPP) for d, r, first, i in joined(h) if d == r]))
     if core not in plans:
         return
     due = {"q0": 1, "q1": 1, "q2": 1}
@@ -157,26 +207,36 @@ def rank_program(g, core, T, topo):
         g.wait_ge(M.sent, sent[0])
         return
 
-    for k in range(5):
+    S.dma_start(T.xs[64:128, :], T.x[64:128, :]).then_inc(M.ld_x, 16)
+    Y.dma_start(T.xs[0:64, :], T.x[0:64, :]).then_inc(M.ld_x, 16)
+    for k in range(4):
         S.dma_start(T.lsend[16 * k:16 * k + 16, :], T.send[:]).then_inc(M.ld_send, 16)
-    for k in range(5, 8):
+    for k in range(4, 8):
         Y.dma_start(T.lsend[16 * k:16 * k + 16, :], T.send[:]).then_inc(M.ld_send, 16)
-    Y.dma_start(T.xs[:], T.x[:]).then_inc(M.ld_x, 16)
+    g.iota(T.rown[:], [[128, 4]], 0, 1).then_inc(M.iot, 1)
+    g.iota(T.skew[:], [[0, NTILE], [1, 16]], 128, -1).then_inc(M.iot, 1)
     g.dma_start(T.lists[0:16, 0:L16], T.mine[:]).then_inc(M.ld_g, 16)
     for k in range(1, 8):
         Y.dma_start(T.lists[16 * k:16 * k + 16, 0:L16], T.mine[:]).then_inc(M.ld_lists, 16)
     for k in range(8):
         Y.dma_start(T.lists[16 * k:16 * k + 16, L16:2 * L16], T.prev[:]).then_inc(M.ld_lists, 16)
-    g.iota(T.places[:], [[1, NT]], 0, 0, allow_small_or_imprecise_dtypes=True).then_inc(M.iot, 1)
-    g.iota(T.pcol[:], [[0, 4]], 0, 1, allow_small_or_imprecise_dtypes=True).then_inc(M.iot, 1)
-    V.memset(T.h0[:, 4 * NBUCK[0] * CAPP:4 * WIDTH[0]], 0.0).then_inc(M.zero, 1)
+    g.iota(T.places[:], [[1, NT]], 0, 0, allow_small_or_imprecise_dtypes=True).then_inc(M.cst, 1)
+    V.memset(T.h0[:, 0:4 * PAD], 0.0).then_inc(M.zero, 1)
     V.memset(T.inv[:], SKIP).then_inc(M.inv0, 1)
+    V.wait_ge(M.iot, 2)
+    V.tensor_scalar(T.low[:], T.skew[:], 15, None, AluOpType.bitwise_and).then_inc(M.one, 1)
+    V.tensor_copy(T.roff[:], T.rown[:]).then_inc(M.cst, 1)
+    V.wait_ge(M.one, 1)
+    V.tensor_scalar(T.diag[:], T.low[:], 0, None, AluOpType.is_equal).then_inc(M.cst, 1)
 
-    V.wait_ge(M.ld_send, 128)
-    for k, ds in enumerate(tiles(rank)):
-        for i, d in enumerate(ds):
+    def offsets(k):
+        for i, d in enumerate(tiles(rank)[k]):
             V.tensor_scalar(T["off%d" % k][:, W16 * i:W16 * i + W16], T.lsend[:, W16 * d:W16 * d + W16], 0, 4,
                             AluOpType.max, AluOpType.mult).then_inc(M["cv%d" % k], 1)
+
+    V.wait_ge(M.ld_send, 128)
+    offsets(0)
+    offsets(1)
 
     def copy(eng, out, src, sem):
         if eng is V:
@@ -185,16 +245,20 @@ def rank_program(g, core, T, topo):
             S.activation(out, src, COPY).then_inc(sem, 1)
 
     V.wait_ge(M.zero, 1)
-    V.wait_ge(M.ld_x, 16)
-    S.wait_ge(M.ld_x, 16)
+    V.wait_ge(M.ld_x, 32)
+    S.wait_ge(M.ld_x, 32)
     for k in range(3):
         n = NBUCK[k] * CAPP
-        for eng, ts in ((V, (0, 1)), (S, (2, 3))):
+        if k == 2:
+            offsets(k)
+        cut = n if k < 2 else 2 * CAPP
+        jobs = ((V, [(0, 0, n), (1, 0, cut)]), (S, [(2, 0, n), (3, 0, n)] + [(1, cut, n)] * (cut < n)))
+        for eng, ts in jobs:
             eng.wait_ge(M["cv%d" % k], NBUCK[k])
-            for t in ts:
-                copy(eng, T["h%d" % k][:, t:4 * n:4],
-                     T.xs[:, t:4 * NT].indirect(T["off%d" % k][:, 0:NBUCK[k] * W16]), M["ga%d" % k])
-        V.wait_ge(M["ga%d" % k], 4)
+            for t, a, b in ts:
+                copy(eng, T["h%d" % k][:, 4 * (WIDTH[k] - n + a) + t:4 * (WIDTH[k] - n + b):4],
+                     T.xs[:, t:4 * NT].indirect(T["off%d" % k][:, a // 16:b // 16]), M["ga%d" % k])
+        V.wait_ge(M["ga%d" % k], 4 + (cut < n))
         q, a = (("q0", 0), ("q1", 0), ("u", MID))[k]
         V.quantize_mx(T[q + "_c"][:, a:a + WIDTH[k]], T[q + "_s"][:, a:a + WIDTH[k]],
                       T["h%d" % k][:]).then_inc(M["q%d" % k], 1)
@@ -203,88 +267,101 @@ def rank_program(g, core, T, topo):
 
     V.wait_ge(M.ld_lists, 240)
     V.wait_ge(M.ld_g, 16)
-    base = [(rank + 1) % N * CAPP, rank * CAPP]
-    half = [slice(0, L16), slice(L16, 2 * L16)]
-    for b, c in zip(base, half):
-        V.tensor_scalar(T.wrap[:, c], T.lists[:, c], b, ARR, AluOpType.is_lt, AluOpType.mult).then_inc(M.wr, 1)
-    V.wait_ge(M.iot, 2)
-    V.tensor_scalar(T.diag[:], T.places[:, 0:128], T.pcol[:, 0:1], None, AluOpType.is_equal).then_inc(M.dia, 1)
-    V.wait_ge(M.wr, 2)
-    V.tensor_tensor(T.turn[:], T.lists[:], T.wrap[:], AluOpType.add).then_inc(M.tu, 1)
-    V.wait_ge(M.tu, 1)
-    for b, c in zip(base, half):
-        V.tensor_scalar(T.moff[:, c], T.turn[:, c], b, None, AluOpType.subtract).then_inc(M.mo, 1)
+    bucket = (rank, (rank - 1) % N)
+    shift = [[slot(rank, d, s) - part(d) - s * CAPP for s in range(N)] for d in bucket]
+    made = [0]
+
+    def term():
+        made[0] += 1
+        return T.terms[:, L16 * (made[0] - 1):L16 * made[0]]
+
+    sums = []
+    for h in range(2):
+        a = T.lists[:, L16 * h:L16 * h + L16]
+        sums.append([a])
+        for s in range(1, N):
+            if shift[h][s] != shift[h][s - 1]:
+                sums[h].append(term())
+                V.tensor_scalar(sums[h][-1], a, s * CAPP, shift[h][s] - shift[h][s - 1], AluOpType.is_ge,
+                                AluOpType.mult).then_inc(M.tm, 1)
+    while max(len(ts) for ts in sums) > 1:
+        V.wait_ge(M.tm, made[0])
+        for h, ts in enumerate(sums):
+            sums[h] = ts[len(ts) // 2 * 2:]
+            for i in range(0, len(ts) - 1, 2):
+                sums[h].append(term())
+                V.tensor_tensor(sums[h][-1], ts[i], ts[i + 1], AluOpType.add).then_inc(M.tm, 1)
+    V.wait_ge(M.tm, made[0])
+    for h in range(2):
+        V.tensor_scalar(T.moff[:, L16 * h:L16 * h + L16], sums[h][0], shift[h][0], None,
+                        AluOpType.add).then_inc(M.mo, 1)
     V.wait_ge(M.mo, 2)
     V.wait_ge(M.inv0, 1)
+    V.wait_ge(M.cst, 3)
     V.tensor_copy(T.inv[:].indirect(T.moff[:, 0:L16]), T.places[:]).then_inc(M.invd, 1)
     V.wait_ge(M.invd, 1)
-    V.wait_ge(M.dia, 1)
+    V.tensor_tensor(T.pick[:], T.inv[:].indirect(T.roff[:, 0:NTILE]), T.diag[:], AluOpType.mult).then_inc(M.pk, 1)
+    V.wait_ge(M.pk, 1)
     for t in range(NTILE):
-        V.tensor_tensor(T.pick[:, 128 * t:128 * t + 128], T.inv[:, 128 * t:128 * t + 128], T.diag[:],
-                        AluOpType.mult).then_inc(M.pk, 1)
-    V.wait_ge(M.pk, NTILE)
-    for t in range(NTILE):
-        V.tensor_reduce(T.idxf[:, t:t + 1], T.pick[:, 128 * t:128 * t + 128], AxisListType.X,
+        V.tensor_reduce(T.idxf[:, t:t + 1], T.pick[:, 16 * t:16 * t + 16], AxisListType.X,
                         AluOpType.add).then_inc(M.ixf, 1)
     V.wait_ge(M.ixf, NTILE)
     V.tensor_copy(T.idx[:, 0:NTILE], T.idxf[:, 0:NTILE]).then_inc(M.ix, 1)
 
-    def product(t, part, a, b, k, sem):
-        P.matmul_mx(T.ps[:, 512 * k:512 * k + b - a], T.u_c[:, 128 * t:128 * t + 128],
-                    T.u_s[:, 128 * t:128 * t + 128], T.u_c[:, part + a:part + b], T.u_s[:, part + a:part + b],
-                    True, True).then_inc(sem, 1)
+    def product(n, t, h, a, b, k, eng):
+        w = slice(part(rank) + 128 * t, part(rank) + 128 * t + 128)
+        m = slice(part(bucket[h]) + a, part(bucket[h]) + b)
+        P.matmul_mx(T.ps[:, 512 * k:512 * k + b - a], T.u_c[:, w], T.u_s[:, w], T.u_c[:, m], T.u_s[:, m],
+                    True, True).then_inc(M["pe%d" % n], 1)
 
-    def leave(eng, t, h, a, b, k, pe):
-        eng.wait_ge(pe, 1)
-        copy(eng, T["raw%d" % t][:, h * ARR + a:h * ARR + b], T.ps[:, 512 * k:512 * k + b - a],
-             M["ev%s%d" % ("op"[h], t)])
+    def leave(n, t, h, a, b, k, eng):
+        eng.wait_ge(M["pe%d" % n], 1)
+        copy(eng, T["raw%d" % t][:, h * ARR + a:h * ARR + b], T.ps[:, 512 * k:512 * k + b - a], M["ev%d%d" % (t, h)])
 
     def order(eng, t, h, a, b, n):
-        eng.wait_ge(M["ev%s%d" % ("op"[h], t)], n)
+        eng.wait_ge(M["ev%d%d" % (t, h)], n)
         win = T["raw%d" % t][:, h * ARR:h * ARR + ARR].indirect(T.moff[:, h * L16 + a // 16:h * L16 + b // 16])
         copy(eng, T["row%d" % t][:, h * NT + a:h * NT + b], win, M["rw%d" % t])
 
-    P.wait_ge(M.q2, 1)
-    for sem in ("hand_c", "hand_s", "own_in"):
-        if sem in due:
-            P.wait_ge(M[sem], due[sem])
+    def landed(*sems):
+        for sem in sems:
+            if sem in due:
+                P.wait_ge(M[sem], due[sem])
+
+    lo = 0 if rank in shared else 1
+    cut = ARR // 2
+    lows = [(0, 0, lo, 0, cut, 0, S), (1, 0, lo, cut, ARR, 1, V)]
+    early = [(2, 0, 1 - lo, 0, 128, 2, V)]
+    late = [(3, 0, 1 - lo, 128, 256, 3, V), (4, 0, 1 - lo, 256, ARR, 4, S)]
+    rest = [(5, 1, 0, 0, ARR, 5, V), (6, 1, 1, 0, ARR, 6, S), (7, 2, 0, 0, ARR, 7, V), (8, 2, 1, 0, ARR, 0, S)]
+    groups = [(("q2", "hand_c", "hand_s", "low_in"), lows), (("q2", "sib_c", "sib_s", "high0"), early)]
+    if lo:
+        groups.reverse()
     S.wait_ge(M.mo, 2)
-    if rank in shared:
-        for t in range(NTILE):
-            product(t, OWN, 0, ARR, t, M["peo%d" % t])
-        P.wait_ge(M.prv_in, due["prv_in"])
-        product(0, PRV, 0, ARR // 2, NTILE, M.pep0)
-        product(0, PRV, ARR // 2, ARR, 2 * NTILE, M.pepx)
-        for t in range(1, NTILE):
-            product(t, PRV, 0, ARR, NTILE + t, M["pep%d" % t])
-        for eng, ts in ((V, (0, 2)), (S, (1,))):
-            for t in ts:
-                leave(eng, t, 0, 0, ARR, t, M["peo%d" % t])
-            for t in ts:
-                order(eng, t, 0, 0, NT, 1)
-        leave(V, 0, 1, 0, ARR // 2, NTILE, M.pep0)
-        leave(S, 0, 1, ARR // 2, ARR, 2 * NTILE, M.pepx)
-        order(V, 0, 1, 0, NT // 2, 2)
-        order(S, 0, 1, NT // 2, NT, 2)
-        for eng, t in ((S, 1), (V, 2)):
-            leave(eng, t, 1, 0, ARR, NTILE + t, M["pep%d" % t])
-            order(eng, t, 1, 0, NT, 1)
-        pieces = [3, 2, 2]
-    else:
-        for t in range(NTILE):
-            product(t, OWN, 0, ARR, t, M["peo%d" % t])
-            if t == 0:
-                P.wait_ge(M.prv_in, due["prv_in"])
-            product(t, PRV, 0, ARR, NTILE + t, M["pep%d" % t])
-        for t in range(NTILE):
-            for eng, h in ((V, 0), (S, 1)):
-                leave(eng, t, h, 0, ARR, h * NTILE + t, M["pe%s%d" % ("op"[h], t)])
-                order(eng, t, h, 0, NT, 1)
-        pieces = [2, 2, 2]
+    for sems, pieces in groups:
+        landed(*sems)
+        for p in pieces:
+            product(*p)
+            leave(*p)
+        if pieces is lows:
+            order(V, 0, lo, 0, NT // 2, 2)
+            order(S, 0, lo, NT // 2, NT, 2)
+    for p in late:
+        landed("high%d" % (p[3] // 128))
+        product(*p)
+        leave(*p)
+    order(V, 0, 1 - lo, 0, NT // 2, 3)
+    order(S, 0, 1 - lo, NT // 2, NT, 3)
+    for p in rest:
+        if p is rest[-1]:
+            P.wait_ge(M["ev0%d" % lo], 2)
+        product(*p)
+        leave(*p)
+        order(p[6], p[1], p[2], 0, NT, 1)
 
     g.wait_ge(M.ix, 1)
     for t in range(NTILE):
-        g.wait_ge(M["rw%d" % t], pieces[t])
+        g.wait_ge(M["rw%d" % t], 2 if t else 4)
         g.indirect_dma_start(T.y[:], IndirectOffsetOnAxis(ap=T.idx[:, t:t + 1], axis=0), T["row%d" % t][:], None,
                              bounds_check=NT - 1, oob_is_err=False).then_inc(M["st%d" % t], 16)
     g.wait_ge(M.sent, sent[0])

from concourse.bass import DstId, RemoteDMATransfer, IndirectOffsetOnAxis
from concourse.mybir import dt, AluOpType, AxisListType, ActivationFunctionType

N, NT, CAPP = 8, 256, 48
ARR = N * CAPP
W16 = CAPP // 16
L16 = NT // 16
NTILE = ARR // 128
SKIP = 1000.0
LOW, MID, HIGH = 0, ARR - CAPP, ARR + CAPP
NBUCK = (2, 3, 3)
WIDTH = (128, 144, 144)
PAD = WIDTH[0] - NBUCK[0] * CAPP

SCRATCH = {
    "xs": ("sbuf", [128, 4 * NT], "bfloat16"),
    "lsend": ("sbuf", [128, N * W16], "int32"),
    "lists": ("sbuf", [128, 2 * L16], "int32"),
    "terms": ("sbuf", [128, 4 * N * L16], "int32"),
    "moff": ("sbuf", [128, 2 * L16], "uint16"),
    "u_c": ("sbuf", [128, HIGH + ARR], "float8_e4m3fn_x4"),
    "u_s": ("sbuf", [128, HIGH + ARR], "uint8"),
    "places": ("sbuf", [128, NT], "float32"),
    "rown": ("sbuf", [128, 4], "int32"),
    "roff": ("sbuf", [128, 4], "uint16"),
    "skew": ("sbuf", [128, 16 * NTILE], "int32"),
    "low": ("sbuf", [128, 16 * NTILE], "int32"),
    "diag": ("sbuf", [128, 16 * NTILE], "float32"),
    "inv": ("sbuf", [128, ARR], "float32"),
    "pick": ("sbuf", [128, 16 * NTILE], "float32"),
    "idxf": ("sbuf", [128, 4], "float32"),
    "idx": ("sbuf", [128, 4], "int32"),
    "ps": ("psum", [128, 512 * 8], "float32"),
}
SEMAPHORES = ["ld_send", "ld_x", "ld_lists", "ld_g", "cst", "iot", "one", "inv0", "zero", "hand_c", "hand_s",
              "rel_c", "rel_s", "join_s", "sib_c", "sib_s", "low_in", "high0", "high1", "high2", "sent", "tm", "mo", "invd", "pk",
              "ixf", "ix"]
for _t in range(3):
    SCRATCH["off%d" % _t] = ("sbuf", [128, 2 * ((NBUCK[_t] * W16 + 1) // 2)], "uint16")
    SCRATCH["h%d" % _t] = ("sbuf", [128, 4 * WIDTH[_t]], "bfloat16")
    SEMAPHORES += ["cv%d" % _t, "ga%d" % _t, "q%d" % _t]
for _t in range(2):
    SCRATCH["q%d_c" % _t] = ("sbuf", [128, WIDTH[_t]], "float8_e4m3fn_x4")
    SCRATCH["q%d_s" % _t] = ("sbuf", [128, WIDTH[_t]], "uint8")
for _t in range(NTILE):
    SCRATCH["raw%d" % _t] = ("sbuf", [128, 2 * ARR], "float32")
    SCRATCH["row%d" % _t] = ("sbuf", [128, 2 * NT], "float32")
    SEMAPHORES += ["ev%d0" % _t, "ev%d1" % _t, "rw%d" % _t, "st%d" % _t]
SEMAPHORES += ["pe%d" % _t for _t in range(9)]


def rank_program(g, core, T, topo):
    V, S, Y, P, M = g.vector, g.scalar, g.sync, g.tensor, T.sem
    COPY = ActivationFunctionType.Copy
    cores = list(T.cores)
    chip = [topo.chip(c) for c in cores]
    shared = [d for d in range(N) if chip[d] == chip[(d + 1) % N]]

    def head(r):
        return r if r in shared else r - 1

    def sib(r):
        return 2 * head(r) + 1 - r

    def wants(d):
        return [d, (d + 1) % N]

    def part(d):
        return LOW if d in shared else HIGH

    def tiles(s):
        far = [d for d in range(N) if all(chip[r] != chip[s] for r in wants(d))]
        far.sort(key=lambda d: (d - s) % N)
        ends = sorted([s, (s - 1) % N], key=part)
        return ([d for d in far if d not in shared], [d for d in far if d in shared],
                ends[:1] + [d for d in range(N) if d not in far + ends] + ends[1:])

    def at(s, d):
        for k, ds in enumerate(tiles(s)):
            if d in ds:
                return (("q0", "q1", "u")[k], ds.index(d) * CAPP + (PAD, 0, MID)[k])

    def helpers(h):
        return [c for c in topo.cores_of(cores[h])
                if topo.die(c) != topo.die(cores[h]) and all(topo.may_write(c, r) for r in cores)]

    def road(h, d, r):
        if d not in tiles(h)[0]:
            return "joined"
        return "direct" if r == d and topo.same_plane(chip[h], chip[r]) else "helper%d" % tiles(h)[0].index(d)

    def relays(h, k):
        return [(c, d, [r for r in wants(d) if road(h, d, r) != "direct"]) for d, c in zip(tiles(h)[0], helpers(h))]

    def senders(r, d):
        if d in shared:
            return [(r + 1 + k) % N for k in range(N)]
        out = [r, sib(r)]
        for way in ("direct", "helper1", "joined", "helper0"):
            for h in shared:
                if h != head(r) and road(h, d, r) == way:
                    out += pair(h, d)
        return out

    def pair(h, d):
        return [h, h + 1] if d in (tiles(h)[0][1], tiles(h)[2][2]) else [h + 1, h]

    def slot(r, d, s):
        return part(d) + senders(r, d).index(s) * CAPP

    def high(r, d, s):
        return "high%d" % ((slot(r, d, s) - HIGH) // 128)

    def joined(h):
        runs = [(d, r) for d in tiles(h)[2] if d not in shared for r in wants(d) if chip[r] != chip[h]]
        return [(d, r, min(slot(r, d, h), slot(r, d, h + 1)), 2 * CAPP * (i + 1)) for i, (d, r) in enumerate(runs)]

    def split(es, n):
        return [es[k * len(es) // n:(k + 1) * len(es) // n] for k in range(n)]

    def plan_rank(s):
        h, o = head(s), sib(s)
        ta, tb, tc = tiles(s)
        off = topo.engines(cores[s], cores[tb[0]])
        near = [e for e in topo.engines(cores[s], cores[o]) if e not in off]
        G = split(off, 4)
        deal = ([G[0] + G[1], G[2], G[3]], [G[2] + G[3], G[0], G[1]])

        def relay(k):
            return [(c, es, ("rel_c", "rel_s")[k]) + at(s, d) + (pair(h, d).index(s) * CAPP, CAPP)
                    for (c, d, _), es in zip(relays(h, k), split(near, 2) if k else (off, near))]

        def direct(k):
            return [(cores[d], off, high(d, d, s)) + at(s, d) + (slot(d, d, s), CAPP)
                    for d in ta if road(h, d, d) == "direct" and (k == 0 or s == h)]

        def heads(k):
            return [(cores[d], es, ("hand_c", "hand_s")[k]) + at(s, d) + (slot(d, d, s), CAPP)
                    for d, es in zip(tb, deal[k])]

        def last(k):
            close = [d for d in tc if o in wants(d)]
            pool = split(near, 2)[0] if k else near
            return ([(cores[o], es, "low_in" if d in shared else ("sib_c", "sib_s")[k]) + at(s, d)
                     + (slot(o, d, s), CAPP) for d, es in zip(close, split(pool, len(close)))] +
                    [(helpers(h)[1], es, "join_s") + at(s, d) + (at_helper + slot(r, d, s) - first, CAPP)
                     for (d, r, first, at_helper), es in zip([j for j in joined(h) if j[0] == j[1]], split(near, 2)[1:])
                     if k])

        calls = [(["q0"], 0, relay(0)), (["q1"], 0, heads(0)), ([], 1, heads(1) + relay(1)),
                 (["q2"], 0, direct(0) + last(0)), ([], 1, direct(1) + last(1))]
        for d, r, first, _ in joined(h):
            if d == tc[2]:
                for k in range(1 + (d != r)):
                    calls.append(([("sib_c", "sib_s")[k]], k,
                                  [(cores[r], off, high(r, d, s), "u", HIGH, first, 2 * CAPP)]))
        for k in range(2 * (s == h)):
            calls.append(([("hand_c", "hand_s")[k]], k,
                          [(cores[o], near, "low_in", "u", LOW + CAPP, LOW, ARR - 2 * CAPP)]))
        return calls

    plans = {cores[s]: plan_rank(s) for s in range(N)}
    for h in shared:
        for k, sem in enumerate(("rel_c", "rel_s")):
            for c, d, rs in relays(h, k):
                s, es = pair(h, d)[0], topo.engines(c, cores[rs[0]])
                plans.setdefault(c, []).append(([sem], k, [
                    (cores[r], e, high(r, d, s), "u", 0, slot(r, d, s), 2 * CAPP)
                    for r, e in zip(rs, split(es, len(rs)))]))
        plans[c].append(([], 1, [(cores[d], es, high(d, d, h + 1), "u", CAPP, slot(d, d, h + 1), CAPP)]))
        plans[helpers(h)[1]].append((["join_s"], 1, [(cores[r], es, "high%d" % ((first - HIGH) // 128), "u", i, first,
                                                      2 * CAPP) for d, r, first, i in joined(h) if d == r]))
    if core not in plans:
        return
    due = {"q0": 1, "q1": 1, "q2": 1}
    for calls in plans.values():
        for _, _, moves in calls:
            for m in moves:
                if m[0] == core:
                    due[m[2]] = due.get(m[2], 0) + len(m[1])
    sent = [0]

    def bits(es):
        m = 0
        for e in es:
            m |= 1 << e
        return m

    def send_all():
        for waits, k, moves in plans[core]:
            for sem in waits:
                g.wait_ge(M[sem], due[sem])
            ts = []
            for dst, es, sem, a, i, j, w in moves:
                src, out = T[a + ("_c", "_s")[k]][:, i:i + w], T["u" + ("_c", "_s")[k]][:, j:j + w]
                if k == 0:
                    src, out = src.bitcast(dt.uint8), out.bitcast(dt.uint8)
                rid, pid = topo.addr(dst)[:2]
                ts.append(RemoteDMATransfer(dst_ids=[DstId(rid=rid, pnc=pid)], dma_engine_mask=bits(es),
                                            remote_sem=M[sem], src=src, dst=out))
                sent[0] += len(es)
            g.remote_dma_fused(ts, local_sem=M.sent)

    rank = T.rank_of(core)
    if rank is None:
        send_all()
        g.wait_ge(M.sent, sent[0])
        return

    S.dma_start(T.xs[64:128, :], T.x[64:128, :]).then_inc(M.ld_x, 16)
    Y.dma_start(T.xs[0:64, :], T.x[0:64, :]).then_inc(M.ld_x, 16)
    for k in range(4):
        S.dma_start(T.lsend[16 * k:16 * k + 16, :], T.send[:]).then_inc(M.ld_send, 16)
    for k in range(4, 8):
        Y.dma_start(T.lsend[16 * k:16 * k + 16, :], T.send[:]).then_inc(M.ld_send, 16)
    g.iota(T.rown[:], [[128, 4]], 0, 1).then_inc(M.iot, 1)
    g.iota(T.skew[:], [[0, NTILE], [1, 16]], 128, -1).then_inc(M.iot, 1)
    g.dma_start(T.lists[0:16, 0:L16], T.mine[:]).then_inc(M.ld_g, 16)
    for k in range(1, 8):
        Y.dma_start(T.lists[16 * k:16 * k + 16, 0:L16], T.mine[:]).then_inc(M.ld_lists, 16)
    for k in range(8):
        Y.dma_start(T.lists[16 * k:16 * k + 16, L16:2 * L16], T.prev[:]).then_inc(M.ld_lists, 16)
    g.iota(T.places[:], [[1, NT]], 0, 0, allow_small_or_imprecise_dtypes=True).then_inc(M.cst, 1)
    V.memset(T.h0[:, 0:4 * PAD], 0.0).then_inc(M.zero, 1)
    V.memset(T.inv[:], SKIP).then_inc(M.inv0, 1)
    V.wait_ge(M.iot, 2)
    V.tensor_scalar(T.low[:], T.skew[:], 15, None, AluOpType.bitwise_and).then_inc(M.one, 1)
    V.tensor_copy(T.roff[:], T.rown[:]).then_inc(M.cst, 1)
    V.wait_ge(M.one, 1)
    V.tensor_scalar(T.diag[:], T.low[:], 0, None, AluOpType.is_equal).then_inc(M.cst, 1)

    def offsets(k):
        for i, d in enumerate(tiles(rank)[k]):
            V.tensor_scalar(T["off%d" % k][:, W16 * i:W16 * i + W16], T.lsend[:, W16 * d:W16 * d + W16], 0, 4,
                            AluOpType.max, AluOpType.mult).then_inc(M["cv%d" % k], 1)

    V.wait_ge(M.ld_send, 128)
    offsets(0)
    offsets(1)

    def copy(eng, out, src, sem):
        if eng is V:
            V.tensor_copy(out, src).then_inc(sem, 1)
        else:
            S.activation(out, src, COPY).then_inc(sem, 1)

    V.wait_ge(M.zero, 1)
    V.wait_ge(M.ld_x, 32)
    S.wait_ge(M.ld_x, 32)
    for k in range(3):
        n = NBUCK[k] * CAPP
        if k == 2:
            offsets(k)
        cut = n if k < 2 else 2 * CAPP
        jobs = ((V, [(0, 0, n), (1, 0, cut)]), (S, [(2, 0, n), (3, 0, n)] + [(1, cut, n)] * (cut < n)))
        for eng, ts in jobs:
            eng.wait_ge(M["cv%d" % k], NBUCK[k])
            for t, a, b in ts:
                copy(eng, T["h%d" % k][:, 4 * (WIDTH[k] - n + a) + t:4 * (WIDTH[k] - n + b):4],
                     T.xs[:, t:4 * NT].indirect(T["off%d" % k][:, a // 16:b // 16]), M["ga%d" % k])
        V.wait_ge(M["ga%d" % k], 4 + (cut < n))
        q, a = (("q0", 0), ("q1", 0), ("u", MID))[k]
        V.quantize_mx(T[q + "_c"][:, a:a + WIDTH[k]], T[q + "_s"][:, a:a + WIDTH[k]],
                      T["h%d" % k][:]).then_inc(M["q%d" % k], 1)

    send_all()

    V.wait_ge(M.ld_lists, 240)
    V.wait_ge(M.ld_g, 16)
    bucket = (rank, (rank - 1) % N)
    shift = [[slot(rank, d, s) - part(d) - s * CAPP for s in range(N)] for d in bucket]
    made = [0]

    def term():
        made[0] += 1
        return T.terms[:, L16 * (made[0] - 1):L16 * made[0]]

    sums = []
    for h in range(2):
        a = T.lists[:, L16 * h:L16 * h + L16]
        sums.append([a])
        for s in range(1, N):
            if shift[h][s] != shift[h][s - 1]:
                sums[h].append(term())
                V.tensor_scalar(sums[h][-1], a, s * CAPP, shift[h][s] - shift[h][s - 1], AluOpType.is_ge,
                                AluOpType.mult).then_inc(M.tm, 1)
    while max(len(ts) for ts in sums) > 1:
        V.wait_ge(M.tm, made[0])
        for h, ts in enumerate(sums):
            sums[h] = ts[len(ts) // 2 * 2:]
            for i in range(0, len(ts) - 1, 2):
                sums[h].append(term())
                V.tensor_tensor(sums[h][-1], ts[i], ts[i + 1], AluOpType.add).then_inc(M.tm, 1)
    V.wait_ge(M.tm, made[0])
    for h in range(2):
        V.tensor_scalar(T.moff[:, L16 * h:L16 * h + L16], sums[h][0], shift[h][0], None,
                        AluOpType.add).then_inc(M.mo, 1)
    V.wait_ge(M.mo, 2)
    V.wait_ge(M.inv0, 1)
    V.wait_ge(M.cst, 3)
    V.tensor_copy(T.inv[:].indirect(T.moff[:, 0:L16]), T.places[:]).then_inc(M.invd, 1)
    V.wait_ge(M.invd, 1)
    V.tensor_tensor(T.pick[:], T.inv[:].indirect(T.roff[:, 0:NTILE]), T.diag[:], AluOpType.mult).then_inc(M.pk, 1)
    V.wait_ge(M.pk, 1)
    for t in range(NTILE):
        V.tensor_reduce(T.idxf[:, t:t + 1], T.pick[:, 16 * t:16 * t + 16], AxisListType.X,
                        AluOpType.add).then_inc(M.ixf, 1)
    V.wait_ge(M.ixf, NTILE)
    V.tensor_copy(T.idx[:, 0:NTILE], T.idxf[:, 0:NTILE]).then_inc(M.ix, 1)

    def product(n, t, h, a, b, k, eng):
        w = slice(part(rank) + 128 * t, part(rank) + 128 * t + 128)
        m = slice(part(bucket[h]) + a, part(bucket[h]) + b)
        P.matmul_mx(T.ps[:, 512 * k:512 * k + b - a], T.u_c[:, w], T.u_s[:, w], T.u_c[:, m], T.u_s[:, m],
                    True, True).then_inc(M["pe%d" % n], 1)

    def leave(n, t, h, a, b, k, eng):
        eng.wait_ge(M["pe%d" % n], 1)
        copy(eng, T["raw%d" % t][:, h * ARR + a:h * ARR + b], T.ps[:, 512 * k:512 * k + b - a], M["ev%d%d" % (t, h)])

    def order(eng, t, h, a, b, n):
        eng.wait_ge(M["ev%d%d" % (t, h)], n)
        win = T["raw%d" % t][:, h * ARR:h * ARR + ARR].indirect(T.moff[:, h * L16 + a // 16:h * L16 + b // 16])
        copy(eng, T["row%d" % t][:, h * NT + a:h * NT + b], win, M["rw%d" % t])

    def landed(*sems):
        for sem in sems:
            if sem in due:
                P.wait_ge(M[sem], due[sem])

    lo = 0 if rank in shared else 1
    cut = ARR // 2
    lows = [(0, 0, lo, 0, cut, 0, S), (1, 0, lo, cut, ARR, 1, V)]
    early = [(2, 0, 1 - lo, 0, 128, 2, V)]
    late = [(3, 0, 1 - lo, 128, 256, 3, V), (4, 0, 1 - lo, 256, ARR, 4, S)]
    rest = [(5, 1, 0, 0, ARR, 5, V), (6, 1, 1, 0, ARR, 6, S), (7, 2, 0, 0, ARR, 7, V), (8, 2, 1, 0, ARR, 0, S)]
    groups = [(("q2", "hand_c", "hand_s", "low_in"), lows), (("q2", "sib_c", "sib_s", "high0"), early)]
    if lo:
        groups.reverse()
    S.wait_ge(M.mo, 2)
    for sems, pieces in groups:
        landed(*sems)
        for p in pieces:
            product(*p)
            leave(*p)
        if pieces is lows:
            order(V, 0, lo, 0, NT // 2, 2)
            order(S, 0, lo, NT // 2, NT, 2)
    for p in late:
        landed("high%d" % (p[3] // 128))
        product(*p)
        leave(*p)
    order(V, 0, 1 - lo, 0, NT // 2, 3)
    order(S, 0, 1 - lo, NT // 2, NT, 3)
    for p in rest:
        if p is rest[-1]:
            P.wait_ge(M["ev0%d" % lo], 2)
        product(*p)
        leave(*p)
        order(p[6], p[1], p[2], 0, NT, 1)

    g.wait_ge(M.ix, 1)
    for t in range(NTILE):
        g.wait_ge(M["rw%d" % t], 2 if t else 4)
        g.indirect_dma_start(T.y[:], IndirectOffsetOnAxis(ap=T.idx[:, t:t + 1], axis=0), T["row%d" % t][:], None,
                             bounds_check=NT - 1, oob_is_err=False).then_inc(M["st%d" % t], 16)
    g.wait_ge(M.sent, sent[0])
    for t in range(NTILE):
        g.wait_ge(M["st%d" % t], 16)
